import numpy as np, ml_dtypes
CORES = [21,85,149,213,277,341,405,469]
N = 8
import mx_ref
NC, WT = 128, 1
LR = np.float32(2.0 ** -3)
BF = ml_dtypes.bfloat16
def cut(t, i, w=512):
    return t[:, w * i:w * i + w]
def tile(rs):
    return np.stack(rs, axis=2).reshape(128, -1).astype(BF)
def pick(b):
    s = np.zeros((128, 128, 4), np.float32)
    s[np.arange(128), np.arange(128), b] = 1.0
    return mx_ref.quantize(s.reshape(128, 512).astype(BF))
def pk(c, s, i=0):
    return (np.ascontiguousarray(c[:, 512 * i:512 * i + 512]), mx_ref.live(s[:, 128 * i:128 * i + 128]))
def inputs(rng, e, E):
    def f(*shape):
        v = (rng.standard_normal(shape, dtype=np.float32) * np.exp2(rng.integers(-2, 3, shape[:-1] + (1,)))).astype(BF)
        return mx_ref.spread((v.astype(np.float32) * np.exp2(rng.integers(-E, E + 1, shape[:-2] + (1, 1))).astype(np.float32)).astype(BF), rng, e)
    def packed(k):
        c = np.zeros((N, 128, k * 512), np.uint8); s = np.zeros((N, 128, k * 128), np.uint8)
        for r in range(N):
            for i in range(k):
                a, b = mx_ref.quantize(f(128, 512)); c[r][:, 512 * i:512 * i + 512] = a; s[r][:, 128 * i:128 * i + 128] = mx_ref.plane(b, rng)
        return c, s
    d = {}
    d["wc"], d["ws"] = packed(WT)
    d["gr"] = f(N, 128, WT * 512)
    d["x"] = f(N, 128, 4 * NC)
    return d
def setup_inputs(rng):
    return inputs(rng, 0, 0)
def setup_inputs_blocks(rng):
    return inputs(rng, 2, 0)
def setup_inputs_wide(rng):
    return inputs(rng, 0, 4)
def setup_inputs_faint(rng):
    d = setup_inputs(rng); d["gr"] = mx_ref.flush((d["gr"].astype(np.float32) * np.float32(2.0 ** -12)).astype(BF))
    return d
def reference(wc, ws, gr, x):
    S = [pick(t) for t in range(4)]
    H = [mx_ref.quantize(tile([mx_ref.matmul(S[t], pk(wc[j], ws[j], i)) - cut(gr[j], i).astype(np.float32)[:, t::4] * LR for t in range(4)])) for j in range(N) for i in range(WT)]
    y = np.zeros((N, 128, N * WT * NC), np.float32)
    for r in range(N):
        X = mx_ref.quantize(x[r])
        for b in range(N * WT):
            y[r][:, NC * b:NC * b + NC] = mx_ref.matmul(H[b], X)
    return {"y": y}

@@ -1,0 +1,184 @@
+from concourse.bass import DstId, RemoteDMATransfer
+from concourse.mybir import dt, AluOpType, ActivationFunctionType
+
+C = 128
+W4 = 4 * C
+NT = 8
+LR = 2.0 ** -3
+
+SCRATCH = {
+    "Z": ("sbuf", [128, W4 + 8], "bfloat16"),
+    "SQ": ("sbuf", [128, 4 * C], "float8_e4m3fn_x4"),
+    "SP": ("sbuf", [128, 4 * C], "uint8"),
+    "WQ": ("sbuf", [128, C], "float8_e4m3fn_x4"),
+    "WP": ("sbuf", [128, C], "uint8"),
+    "G": ("sbuf", [128, W4], "bfloat16"),
+    "G8": ("sbuf", [128, W4], "bfloat16"),
+    "H": ("sbuf", [128, W4], "bfloat16"),
+    "XT": ("sbuf", [128, W4], "bfloat16"),
+    "XQ": ("sbuf", [128, C], "float8_e4m3fn_x4"),
+    "XP": ("sbuf", [128, C], "uint8"),
+    "Q": ("sbuf", [128, NT * C], "float8_e4m3fn_x4"),
+    "P": ("sbuf", [128, NT * C], "uint8"),
+    "Y": ("sbuf", [128, NT * C], "float32"),
+    "ps": ("psum", [128, NT * 512], "float32"),
+}
+SEMAPHORES = (["z0", "z1", "sq", "lw", "lg", "lx", "h", "vq", "xq", "sent", "issued", "stored",
+               "rp1", "rp2", "rc12", "rc3", "rk1", "rkp", "rk2"]
+              + ["d%d" % b for b in range(4)] + ["g%d" % b for b in range(4)]
+              + ["m%d" % k for k in range(NT)] + ["yn", "y45", "y6", "y7"])
+
+
+def rack_group(core, T, topo):
+    def at(same_host, same_chip):
+        return [c for c in T.cores if topo.rack(topo.host(c)) == topo.rack(topo.host(core))
+                and (topo.host(c) == topo.host(core)) == same_host
+                and (topo.chip(c) == topo.chip(core)) == same_chip][0]
+    return [at(True, True), at(True, False), at(False, True), at(False, False)]
+
+
+def rank_program(g, core, T, topo):
+    rank = T.rank_of(core)
+    if rank is None:
+        return
+    s = T.sem
+    near = rack_group(core, T, topo)
+    peer = [c for c in T.cores if topo.rack(topo.host(c)) != topo.rack(topo.host(core))
+            and topo.chip(c) == topo.chip(core) and topo.may_write(core, c)][0]
+    owner = near + rack_group(peer, T, topo)
+
+    def codes(a, b):
+        return T.Q[:, a * C:b * C].bitcast(dt.uint8)
+
+    def planes(a, b):
+        return T.P[:, a * C:b * C]
+
+    def yblk(k):
+        r = T.rank_of(owner[k])
+        return r * C, (r + 1) * C
+
+    def bank(k):
+        return ((k + 4) % NT) * 512
+
+    g.sync.dma_start(T.WQ[:, 0:C].bitcast(dt.uint8), T.wc[:, :]).then_inc(s.lw, 16)
+    g.sync.dma_start(T.WP[:, :], T.ws[:, :]).then_inc(s.lw, 16)
+    g.sync.wait_ge(s.sq, 4)
+    g.sync.dma_start(T.XT[:, :], T.x[:, :]).then_inc(s.lx, 16)
+
+    g.scalar.dma_start(T.G[:, :], T.gr[:, :]).then_inc(s.lg, 16)
+    g.scalar.wait_ge(s.lg, 16)
+    for b in range(4):
+        g.scalar.activation(T.G8[:, b * C:(b + 1) * C], T.G[:, b:W4:4], ActivationFunctionType.Copy,
+                            scale=LR).then_inc(s["g%d" % b], 1)
+
+    g.vector.memset(T.Z[:, :], 0.0).then_inc(s.z0, 1)
+    g.wait_ge(s.z0, 1)
+    g.affine_select(T.Z[:, 3:3 + W4:4], T.Z[:, 3:3 + W4:4], [[-1, C]], AluOpType.not_equal, 1.0, 0, 1).then_inc(s.z1, 1)
+    g.vector.wait_ge(s.z1, 1)
+    for b in range(4):
+        g.vector.quantize_mx(T.SQ[:, b * C:(b + 1) * C], T.SP[:, b * C:(b + 1) * C],
+                             T.Z[:, 3 - b:3 - b + W4]).then_inc(s.sq, 1)
+
+    g.tensor.wait_ge(s.sq, 4)
+    g.tensor.wait_ge(s.lw, 32)
+    for b in range(4):
+        g.tensor.matmul_mx(T.ps[:, b * 512:b * 512 + C], T.SQ[:, b * C:(b + 1) * C], T.SP[:, b * C:(b + 1) * C],
+                           T.WQ[:, 0:C], T.WP[:, 0:C], True, True).then_inc(s["d%d" % b], 1)
+
+    for b in range(4):
+        g.vector.wait_ge(s["d%d" % b], 1)
+        g.vector.wait_ge(s["g%d" % b], 1)
+        g.vector.tensor_tensor(T.H[:, b:W4:4], T.ps[:, b * 512:b * 512 + C], T.G8[:, b * C:(b + 1) * C],
+                               AluOpType.subtract).then_inc(s.h, 1)
+    g.vector.wait_ge(s.h, 4)
+    g.vector.quantize_mx(T.Q[:, 0:C], T.P[:, 0:C], T.H[:, :]).then_inc(s.vq, 1)
+    g.vector.wait_ge(s.lx, 16)
+    g.vector.quantize_mx(T.XQ[:, :], T.XP[:, :], T.XT[:, :]).then_inc(s.xq, 1)
+
+    sends = [0]
+
+    def send(dst, src, what, a, to, sem):
+        mask = topo.mask(core, to[0][0])
+        for d, _ in to:
+            mask &= topo.mask(core, d)
+        n = bin(mask).count("1")
+        if len(to) == 1:
+            rid, pid = topo.addr(to[0][0], core)
+            g.remote_dma(out_ap=dst[0], in_ap=src, remote_sem=sem, local_sem=s.sent, pid=pid, routing_id=rid,
+                         dma_engine_mask=mask)
+        else:
+            ids = []
+            for d, _ in to:
+                rid, pid = topo.addr(d, core)
+                ids.append(DstId(rid=rid, pnc=pid))
+            g.remote_dma_fused([RemoteDMATransfer(dst_ids=ids, dma_engine_mask=mask, remote_sem=sem, srcs=[src], dsts=dst)],
+                               local_sem=s.sent)
+        sends[0] += n
+        return n
+
+    def put(what, a, b, to, sem):
+        return send([what(k, k + b - a) for _, k in to], what(a, b), what, a, to, sem)
+
+    g.wait_ge(s.vq, 1)
+    n = put(planes, 0, 1, [(near[1], 1)], s.rp1)
+    put(codes, 0, 1, [(near[1], 1), (near[2], 2)], s.rc12)
+    g.wait_ge(s.rp1, n)
+    put(planes, 0, 2, [(near[2], 2)], s.rp2)
+    put(codes, 0, 1, [(near[3], 3)], s.rc3)
+    g.wait_ge(s.rc12, 2 * n)
+    m = put(codes, 0, 3, [(peer, 4)], s.rk1)
+    g.wait_ge(s.rp2, n)
+    put(planes, 0, 4, [(peer, 4)], s.rkp)
+    g.wait_ge(s.rc3, n)
+    put(codes, 3, 4, [(peer, 7)], s.rk2)
+    g.sem_inc(s.issued, 1)
+    g.wait_ge(s.sent, sends[0])
+
+    def product(k):
+        g.tensor.matmul_mx(T.ps[:, bank(k):bank(k) + C], T.Q[:, k * C:(k + 1) * C], T.P[:, k * C:(k + 1) * C],
+                           T.XQ[:, :], T.XP[:, :], True, True).then_inc(s["m%d" % k], 1)
+
+    g.tensor.wait_ge(s.vq, 1)
+    g.tensor.wait_ge(s.xq, 1)
+    product(0)
+    g.tensor.wait_ge(s.rp1, n)
+    g.tensor.wait_ge(s.rc12, 2 * n)
+    product(1)
+    g.tensor.wait_ge(s.rp2, n)
+    product(2)
+    g.tensor.wait_ge(s.rc3, n)
+    product(3)
+    g.tensor.wait_ge(s.h, 4)
+    g.tensor.wait_ge(s.rk1, m)
+    g.tensor.wait_ge(s.rkp, m)
+    product(4)
+    product(5)
+    product(6)
+    g.tensor.wait_ge(s.rk2, m)
+    product(7)
+
+    for k in range(NT):
+        a, b = yblk(k)
+        done = s.yn if k < 4 else s.y45 if k < 6 else s["y%d" % k]
+        if k % 2 == 0 or k == 7:
+            g.vector.wait_ge(s["m%d" % k], 1)
+            g.vector.tensor_copy(T.Y[:, a:b], T.ps[:, bank(k):bank(k) + C]).then_inc(done, 1)
+        else:
+            g.scalar.wait_ge(s["m%d" % k], 1)
+            g.scalar.activation(T.Y[:, a:b], T.ps[:, bank(k):bank(k) + C], ActivationFunctionType.Copy).then_inc(done, 1)
+
+    def store(ks):
+        cols = [yblk(k) for k in ks]
+        a, b = min(c[0] for c in cols), max(c[1] for c in cols)
+        g.sync.dma_start(T.y[:, a:b], T.Y[:, a:b]).then_inc(s.stored, 16)
+
+    g.sync.wait_ge(s.issued, 1)
+    g.sync.wait_ge(s.yn, 4)
+    store([0, 1, 2, 3])
+    g.sync.wait_ge(s.y45, 2)
+    store([4, 5])
+    g.sync.wait_ge(s.y6, 1)
+    store([6])
+    g.sync.wait_ge(s.y7, 1)
+    store([7])
+    g.sync.wait_ge(s.stored, 64)

@@ -5,6 +5,8 @@ C = 128
 W4 = 4 * C
 NT = 8
 LR = 2.0 ** -3
+QP = {2: 0, 3: 1, 0: 2, 4: 3, 1: 4, 5: 5, 6: 6, 7: 7}
+PP = {0: 0, 4: 1, 1: 2, 5: 3, 2: 4, 6: 5, 3: 6, 7: 7}
 
 SCRATCH = {
     "Z": ("sbuf", [128, W4 + 8], "bfloat16"),
@@ -24,9 +26,8 @@ SCRATCH = {
     "ps": ("psum", [128, NT * 512], "float32"),
 }
 SEMAPHORES = (["z0", "z1", "sq", "lw", "lg", "lx", "h", "vq", "xq", "sent", "issued", "stored",
-               "rp1", "rp2", "rc12", "rc3", "rk1", "rkp", "rk2"]
-              + ["d%d" % b for b in range(4)] + ["g%d" % b for b in range(4)]
-              + ["m%d" % k for k in range(NT)] + ["yn", "y45", "y6", "y7"])
+               "rp4", "rp1", "rp3", "rc4", "rc23", "rm1", "rk", "yn", "y45", "y67"]
+              + ["d%d" % b for b in range(4)] + ["g%d" % b for b in range(4)] + ["m%d" % k for k in range(NT)])
 
 
 def rack_group(core, T, topo):
@@ -47,11 +48,11 @@ def rank_program(g, core, T, topo):
             and topo.chip(c) == topo.chip(core) and topo.may_write(core, c)][0]
     owner = near + rack_group(peer, T, topo)
 
-    def codes(a, b):
-        return T.Q[:, a * C:b * C].bitcast(dt.uint8)
+    def codes(a, n=1):
+        return T.Q[:, QP[a] * C:(QP[a] + n) * C].bitcast(dt.uint8)
 
-    def planes(a, b):
-        return T.P[:, a * C:b * C]
+    def planes(a, n=1):
+        return T.P[:, PP[a] * C:(PP[a] + n) * C]
 
     def yblk(k):
         r = T.rank_of(owner[k])
@@ -91,76 +92,71 @@ def rank_program(g, core, T, topo):
         g.vector.tensor_tensor(T.H[:, b:W4:4], T.ps[:, b * 512:b * 512 + C], T.G8[:, b * C:(b + 1) * C],
                                AluOpType.subtract).then_inc(s.h, 1)
     g.vector.wait_ge(s.h, 4)
-    g.vector.quantize_mx(T.Q[:, 0:C], T.P[:, 0:C], T.H[:, :]).then_inc(s.vq, 1)
+    g.vector.quantize_mx(T.Q[:, QP[0] * C:(QP[0] + 1) * C], planes(0), T.H[:, :]).then_inc(s.vq, 1)
     g.vector.wait_ge(s.lx, 16)
     g.vector.quantize_mx(T.XQ[:, :], T.XP[:, :], T.XT[:, :]).then_inc(s.xq, 1)
 
     sends = [0]
 
-    def send(dst, src, what, a, to, sem):
+    def put(what, a, n, to, sem):
         mask = topo.mask(core, to[0][0])
         for d, _ in to:
             mask &= topo.mask(core, d)
-        n = bin(mask).count("1")
+        ids = [topo.addr(d, core) for d, _ in to]
+        dsts = [what(k, n) for _, k in to]
         if len(to) == 1:
-            rid, pid = topo.addr(to[0][0], core)
-            g.remote_dma(out_ap=dst[0], in_ap=src, remote_sem=sem, local_sem=s.sent, pid=pid, routing_id=rid,
-                         dma_engine_mask=mask)
+            g.remote_dma(out_ap=dsts[0], in_ap=what(a, n), remote_sem=sem, local_sem=s.sent, pid=ids[0][1],
+                         routing_id=ids[0][0], dma_engine_mask=mask)
         else:
-            ids = []
-            for d, _ in to:
-                rid, pid = topo.addr(d, core)
-                ids.append(DstId(rid=rid, pnc=pid))
-            g.remote_dma_fused([RemoteDMATransfer(dst_ids=ids, dma_engine_mask=mask, remote_sem=sem, srcs=[src], dsts=dst)],
-                               local_sem=s.sent)
-        sends[0] += n
-        return n
-
-    def put(what, a, b, to, sem):
-        return send([what(k, k + b - a) for _, k in to], what(a, b), what, a, to, sem)
+            g.remote_dma_fused([RemoteDMATransfer(dst_ids=[DstId(rid=r, pnc=p) for r, p in ids], dma_engine_mask=mask,
+                                                  remote_sem=sem, srcs=[what(a, n)], dsts=dsts)], local_sem=s.sent)
+        engines = bin(mask).count("1")
+        sends[0] += engines
+        return engines
 
     g.wait_ge(s.vq, 1)
-    n = put(planes, 0, 1, [(near[1], 1)], s.rp1)
-    put(codes, 0, 1, [(near[1], 1), (near[2], 2)], s.rc12)
-    g.wait_ge(s.rp1, n)
-    put(planes, 0, 2, [(near[2], 2)], s.rp2)
-    put(codes, 0, 1, [(near[3], 3)], s.rc3)
-    g.wait_ge(s.rc12, 2 * n)
-    m = put(codes, 0, 3, [(peer, 4)], s.rk1)
-    g.wait_ge(s.rp2, n)
-    put(planes, 0, 4, [(peer, 4)], s.rkp)
-    g.wait_ge(s.rc3, n)
-    put(codes, 3, 4, [(peer, 7)], s.rk2)
+    ec = put(planes, 0, 1, [(peer, 4)], s.rp4)
+    put(codes, 0, 1, [(peer, 4)], s.rc4)
+    es = put(codes, 0, 1, [(near[2], 2), (near[3], 3)], s.rc23)
+    g.wait_ge(s.rp4, ec)
+    put(planes, 0, 2, [(near[1], 1)], s.rp1)
+    g.wait_ge(s.rc4, ec)
+    put(codes, 0, 2, [(near[1], 1)], s.rm1)
+    g.wait_ge(s.rc23, 2 * es)
+    put(codes, 2, 2, [(peer, 6)], s.rk)
+    g.wait_ge(s.rp1, es)
+    put(planes, 0, 4, [(near[2], 2)], s.rp3)
     g.sem_inc(s.issued, 1)
     g.wait_ge(s.sent, sends[0])
 
     def product(k):
-        g.tensor.matmul_mx(T.ps[:, bank(k):bank(k) + C], T.Q[:, k * C:(k + 1) * C], T.P[:, k * C:(k + 1) * C],
+        q, p = QP[k], PP[k]
+        g.tensor.matmul_mx(T.ps[:, bank(k):bank(k) + C], T.Q[:, q * C:(q + 1) * C], T.P[:, p * C:(p + 1) * C],
                            T.XQ[:, :], T.XP[:, :], True, True).then_inc(s["m%d" % k], 1)
 
     g.tensor.wait_ge(s.vq, 1)
     g.tensor.wait_ge(s.xq, 1)
     product(0)
-    g.tensor.wait_ge(s.rp1, n)
-    g.tensor.wait_ge(s.rc12, 2 * n)
-    product(1)
-    g.tensor.wait_ge(s.rp2, n)
-    product(2)
-    g.tensor.wait_ge(s.rc3, n)
-    product(3)
     g.tensor.wait_ge(s.h, 4)
-    g.tensor.wait_ge(s.rk1, m)
-    g.tensor.wait_ge(s.rkp, m)
+    g.tensor.wait_ge(s.rp4, ec)
+    g.tensor.wait_ge(s.rc4, ec)
     product(4)
+    g.tensor.wait_ge(s.rp1, es)
+    g.tensor.wait_ge(s.rm1, es)
+    product(1)
     product(5)
+    g.tensor.wait_ge(s.rc23, 2 * es)
+    g.tensor.wait_ge(s.rp3, es)
+    product(2)
+    product(3)
+    g.tensor.wait_ge(s.rk, ec)
     product(6)
-    g.tensor.wait_ge(s.rk2, m)
     product(7)
 
-    for k in range(NT):
+    for k in (0, 4, 1, 5, 2, 3, 6, 7):
         a, b = yblk(k)
-        done = s.yn if k < 4 else s.y45 if k < 6 else s["y%d" % k]
-        if k % 2 == 0 or k == 7:
+        done = s.yn if k < 4 else s.y45 if k < 6 else s.y67
+        if k in (0, 1, 2, 6):
             g.vector.wait_ge(s["m%d" % k], 1)
             g.vector.tensor_copy(T.Y[:, a:b], T.ps[:, bank(k):bank(k) + C]).then_inc(done, 1)
         else:
@@ -173,12 +169,10 @@ def rank_program(g, core, T, topo):
         g.sync.dma_start(T.y[:, a:b], T.Y[:, a:b]).then_inc(s.stored, 16)
 
     g.sync.wait_ge(s.issued, 1)
-    g.sync.wait_ge(s.yn, 4)
-    store([0, 1, 2, 3])
     g.sync.wait_ge(s.y45, 2)
     store([4, 5])
-    g.sync.wait_ge(s.y6, 1)
-    store([6])
-    g.sync.wait_ge(s.y7, 1)
-    store([7])
-    g.sync.wait_ge(s.stored, 64)
+    g.sync.wait_ge(s.yn, 4)
+    store([0, 1, 2, 3])
+    g.sync.wait_ge(s.y67, 2)
+    store([6, 7])
+    g.sync.wait_ge(s.stored, 48)

@@ -5,8 +5,9 @@ C = 128
 W4 = 4 * C
 NT = 8
 LR = 2.0 ** -3
-QP = {2: 0, 3: 1, 0: 2, 4: 3, 1: 4, 5: 5, 6: 6, 7: 7}
+QP = {0: 0, 4: 1, 3: 2, 7: 3, 1: 4, 5: 5, 2: 6, 6: 7}
 PP = {0: 0, 4: 1, 1: 2, 5: 3, 2: 4, 6: 5, 3: 6, 7: 7}
+STORES = {"y01": [0, 1], "y45": [4, 5], "y23": [2, 3], "y7": [7], "y6": [6]}
 
 SCRATCH = {
     "Z": ("sbuf", [128, W4 + 8], "bfloat16"),
@@ -26,7 +27,7 @@ SCRATCH = {
     "ps": ("psum", [128, NT * 512], "float32"),
 }
 SEMAPHORES = (["z0", "z1", "sq", "lw", "lg", "lx", "h", "vq", "xq", "sent", "issued", "stored",
-               "rp4", "rp1", "rp3", "rc4", "rc23", "rm1", "rk", "yn", "y45", "y67"]
+               "rp4", "rp1", "rp3", "rc4", "rc12", "rm3", "rk5", "rr6"] + list(STORES)
               + ["d%d" % b for b in range(4)] + ["g%d" % b for b in range(4)] + ["m%d" % k for k in range(NT)])
 
 
@@ -117,15 +118,16 @@ def rank_program(g, core, T, topo):
     g.wait_ge(s.vq, 1)
     ec = put(planes, 0, 1, [(peer, 4)], s.rp4)
     put(codes, 0, 1, [(peer, 4)], s.rc4)
-    es = put(codes, 0, 1, [(near[2], 2), (near[3], 3)], s.rc23)
+    es = put(codes, 0, 1, [(near[1], 1), (near[2], 2)], s.rc12)
     g.wait_ge(s.rp4, ec)
     put(planes, 0, 2, [(near[1], 1)], s.rp1)
     g.wait_ge(s.rc4, ec)
-    put(codes, 0, 2, [(near[1], 1)], s.rm1)
-    g.wait_ge(s.rc23, 2 * es)
-    put(codes, 2, 2, [(peer, 6)], s.rk)
+    put(codes, 0, 2, [(near[3], 3)], s.rm3)
+    g.wait_ge(s.rc12, 2 * es)
+    put(codes, 1, 1, [(peer, 5)], s.rk5)
     g.wait_ge(s.rp1, es)
     put(planes, 0, 4, [(near[2], 2)], s.rp3)
+    put(codes, 4, 1, [(near[2], 6)], s.rr6)
     g.sem_inc(s.issued, 1)
     g.wait_ge(s.sent, sends[0])
 
@@ -142,37 +144,33 @@ def rank_program(g, core, T, topo):
     g.tensor.wait_ge(s.rc4, ec)
     product(4)
     g.tensor.wait_ge(s.rp1, es)
-    g.tensor.wait_ge(s.rm1, es)
+    g.tensor.wait_ge(s.rc12, 2 * es)
     product(1)
+    g.tensor.wait_ge(s.rk5, ec)
     product(5)
-    g.tensor.wait_ge(s.rc23, 2 * es)
+    g.tensor.wait_ge(s.rm3, es)
     g.tensor.wait_ge(s.rp3, es)
     product(2)
     product(3)
-    g.tensor.wait_ge(s.rk, ec)
-    product(6)
     product(7)
+    g.tensor.wait_ge(s.rr6, es)
+    product(6)
 
-    for k in (0, 4, 1, 5, 2, 3, 6, 7):
+    ready = {k: n for n in STORES for k in STORES[n]}
+    for k in (0, 4, 1, 5, 2, 3, 7, 6):
         a, b = yblk(k)
-        done = s.yn if k < 4 else s.y45 if k < 6 else s.y67
         if k in (0, 1, 2, 6):
             g.vector.wait_ge(s["m%d" % k], 1)
-            g.vector.tensor_copy(T.Y[:, a:b], T.ps[:, bank(k):bank(k) + C]).then_inc(done, 1)
+            g.vector.tensor_copy(T.Y[:, a:b], T.ps[:, bank(k):bank(k) + C]).then_inc(s[ready[k]], 1)
         else:
             g.scalar.wait_ge(s["m%d" % k], 1)
-            g.scalar.activation(T.Y[:, a:b], T.ps[:, bank(k):bank(k) + C], ActivationFunctionType.Copy).then_inc(done, 1)
-
-    def store(ks):
-        cols = [yblk(k) for k in ks]
-        a, b = min(c[0] for c in cols), max(c[1] for c in cols)
-        g.sync.dma_start(T.y[:, a:b], T.Y[:, a:b]).then_inc(s.stored, 16)
+            g.scalar.activation(T.Y[:, a:b], T.ps[:, bank(k):bank(k) + C],
+                                ActivationFunctionType.Copy).then_inc(s[ready[k]], 1)
 
     g.sync.wait_ge(s.issued, 1)
-    g.sync.wait_ge(s.y45, 2)
-    store([4, 5])
-    g.sync.wait_ge(s.yn, 4)
-    store([0, 1, 2, 3])
-    g.sync.wait_ge(s.y67, 2)
-    store([6, 7])
-    g.sync.wait_ge(s.stored, 48)
+    for n in STORES:
+        cols = [yblk(k) for k in STORES[n]]
+        a, b = min(c[0] for c in cols), max(c[1] for c in cols)
+        g.sync.wait_ge(s[n], len(cols))
+        g.sync.dma_start(T.y[:, a:b], T.Y[:, a:b]).then_inc(s.stored, 16)
+    g.sync.wait_ge(s.stored, 16 * len(STORES))

@@ -4,10 +4,10 @@ from concourse.mybir import dt, AluOpType, ActivationFunctionType
 C = 128
 W4 = 4 * C
 NT = 8
+WORLD = 512
 LR = 2.0 ** -3
-QP = {0: 0, 4: 1, 3: 2, 7: 3, 1: 4, 5: 5, 2: 6, 6: 7}
 PP = {0: 0, 4: 1, 1: 2, 5: 3, 2: 4, 6: 5, 3: 6, 7: 7}
-STORES = {"y01": [0, 1], "y45": [4, 5], "y23": [2, 3], "y7": [7], "y6": [6]}
+STORES = {"y01": [0, 1], "y45": [4, 5], "y23": [2, 3], "y67": [6, 7]}
 
 SCRATCH = {
     "Z": ("sbuf", [128, W4 + 8], "bfloat16"),
@@ -23,12 +23,13 @@ SCRATCH = {
     "XP": ("sbuf", [128, C], "uint8"),
     "Q": ("sbuf", [128, NT * C], "float8_e4m3fn_x4"),
     "P": ("sbuf", [128, NT * C], "uint8"),
+    "HQ": ("sbuf", [128, C], "float8_e4m3fn_x4"),
     "Y": ("sbuf", [128, NT * C], "float32"),
     "ps": ("psum", [128, NT * 512], "float32"),
 }
-SEMAPHORES = (["z0", "z1", "sq", "lw", "lg", "lx", "h", "vq", "xq", "sent", "issued", "stored",
-               "rp4", "rp1", "rp3", "rc4", "rc12", "rm3", "rk5", "rr6"] + list(STORES)
-              + ["d%d" % b for b in range(4)] + ["g%d" % b for b in range(4)] + ["m%d" % k for k in range(NT)])
+SEMAPHORES = (["z0", "z1", "z2", "lw", "lg", "lx", "h", "vq", "xq", "sent", "issued", "stored",
+               "rp4", "rp", "rc4", "rc12", "rc3", "rc5", "rc67", "rh"] + list(STORES)
+              + [n + "%d" % b for n in ("sq", "d", "g") for b in range(4)] + ["m%d" % k for k in range(NT)])
 
 
 def rack_group(core, T, topo):
@@ -39,18 +40,61 @@ def rack_group(core, T, topo):
     return [at(True, True), at(True, False), at(False, True), at(False, False)]
 
 
+def peer_of(core, T, topo):
+    return [c for c in T.cores if topo.rack(topo.host(c)) != topo.rack(topo.host(core))
+            and topo.chip(c) == topo.chip(core) and topo.may_write(core, c)][0]
+
+
+def helper_of(core, topo):
+    return [c for c in range(WORLD) if topo.host(c) == topo.host(core) and topo.chip(c) == topo.chip(core)
+            and topo.die(c) != topo.die(core)][0]
+
+
+def send(g, core, topo, sem, local, src, to, mask):
+    ids = [topo.addr(d, core) for d, _ in to]
+    dsts = [ap for _, ap in to]
+    if len(to) == 1:
+        g.remote_dma(out_ap=dsts[0], in_ap=src, remote_sem=sem, local_sem=local, pid=ids[0][1],
+                     routing_id=ids[0][0], dma_engine_mask=mask)
+    else:
+        g.remote_dma_fused([RemoteDMATransfer(dst_ids=[DstId(rid=r, pnc=p) for r, p in ids], dma_engine_mask=mask,
+                                              remote_sem=sem, srcs=[src], dsts=dsts)], local_sem=local)
+    return bin(mask).count("1")
+
+
+def chip_mask(core, helper, away, topo):
+    return topo.mask(core, helper) & ~topo.mask(core, away)
+
+
+def helper_program(g, core, owner, T, topo):
+    s = T.sem
+    near = rack_group(owner, T, topo)
+    far = rack_group(peer_of(owner, T, topo), T, topo)
+    g.wait_ge(s.rh, bin(chip_mask(owner, core, far[0], topo)).count("1"))
+    src = T.HQ[:, 0:C].bitcast(dt.uint8)
+    n = 0
+    for to, k, sem in ((far[1], 5, s.rc5), (near[3], 3, s.rc3)):
+        n += send(g, core, topo, sem, s.sent, src, [(to, T.Q[:, k * C:(k + 1) * C].bitcast(dt.uint8))],
+                  topo.mask(core, to))
+    g.wait_ge(s.sent, n)
+
+
 def rank_program(g, core, T, topo):
     rank = T.rank_of(core)
     if rank is None:
+        for c in T.cores:
+            if topo.host(c) == topo.host(core) and topo.chip(c) == topo.chip(core) and helper_of(c, topo) == core:
+                helper_program(g, core, c, T, topo)
         return
     s = T.sem
     near = rack_group(core, T, topo)
-    peer = [c for c in T.cores if topo.rack(topo.host(c)) != topo.rack(topo.host(core))
-            and topo.chip(c) == topo.chip(core) and topo.may_write(core, c)][0]
-    owner = near + rack_group(peer, T, topo)
+    peer = peer_of(core, T, topo)
+    far = rack_group(peer, T, topo)
+    helper = helper_of(core, topo)
+    owner = near + far
 
-    def codes(a, n=1):
-        return T.Q[:, QP[a] * C:(QP[a] + n) * C].bitcast(dt.uint8)
+    def codes(a):
+        return T.Q[:, a * C:(a + 1) * C].bitcast(dt.uint8)
 
     def planes(a, n=1):
         return T.P[:, PP[a] * C:(PP[a] + n) * C]
@@ -64,7 +108,7 @@ def rank_program(g, core, T, topo):
 
     g.sync.dma_start(T.WQ[:, 0:C].bitcast(dt.uint8), T.wc[:, :]).then_inc(s.lw, 16)
     g.sync.dma_start(T.WP[:, :], T.ws[:, :]).then_inc(s.lw, 16)
-    g.sync.wait_ge(s.sq, 4)
+    g.sync.wait_ge(s.sq3, 1)
     g.sync.dma_start(T.XT[:, :], T.x[:, :]).then_inc(s.lx, 16)
 
     g.scalar.dma_start(T.G[:, :], T.gr[:, :]).then_inc(s.lg, 16)
@@ -73,17 +117,20 @@ def rank_program(g, core, T, topo):
         g.scalar.activation(T.G8[:, b * C:(b + 1) * C], T.G[:, b:W4:4], ActivationFunctionType.Copy,
                             scale=LR).then_inc(s["g%d" % b], 1)
 
-    g.vector.memset(T.Z[:, :], 0.0).then_inc(s.z0, 1)
+    g.vector.memset(T.Z[:, 3:3 + W4:4], 0.0).then_inc(s.z0, 1)
+    for k in range(3):
+        g.vector.memset(T.Z[:, k:W4 + 3:4], 0.0).then_inc(s.z2, 1)
     g.wait_ge(s.z0, 1)
     g.affine_select(T.Z[:, 3:3 + W4:4], T.Z[:, 3:3 + W4:4], [[-1, C]], AluOpType.not_equal, 1.0, 0, 1).then_inc(s.z1, 1)
+    g.vector.wait_ge(s.z2, 3)
     g.vector.wait_ge(s.z1, 1)
     for b in range(4):
         g.vector.quantize_mx(T.SQ[:, b * C:(b + 1) * C], T.SP[:, b * C:(b + 1) * C],
-                             T.Z[:, 3 - b:3 - b + W4]).then_inc(s.sq, 1)
+                             T.Z[:, 3 - b:3 - b + W4]).then_inc(s["sq%d" % b], 1)
 
-    g.tensor.wait_ge(s.sq, 4)
     g.tensor.wait_ge(s.lw, 32)
     for b in range(4):
+        g.tensor.wait_ge(s["sq%d" % b], 1)
         g.tensor.matmul_mx(T.ps[:, b * 512:b * 512 + C], T.SQ[:, b * C:(b + 1) * C], T.SP[:, b * C:(b + 1) * C],
                            T.WQ[:, 0:C], T.WP[:, 0:C], True, True).then_inc(s["d%d" % b], 1)
 
@@ -93,47 +140,30 @@ def rank_program(g, core, T, topo):
         g.vector.tensor_tensor(T.H[:, b:W4:4], T.ps[:, b * 512:b * 512 + C], T.G8[:, b * C:(b + 1) * C],
                                AluOpType.subtract).then_inc(s.h, 1)
     g.vector.wait_ge(s.h, 4)
-    g.vector.quantize_mx(T.Q[:, QP[0] * C:(QP[0] + 1) * C], planes(0), T.H[:, :]).then_inc(s.vq, 1)
+    g.vector.quantize_mx(T.Q[:, 0:C], planes(0), T.H[:, :]).then_inc(s.vq, 1)
     g.vector.wait_ge(s.lx, 16)
     g.vector.quantize_mx(T.XQ[:, :], T.XP[:, :], T.XT[:, :]).then_inc(s.xq, 1)
 
-    sends = [0]
-
-    def put(what, a, n, to, sem):
-        mask = topo.mask(core, to[0][0])
-        for d, _ in to:
-            mask &= topo.mask(core, d)
-        ids = [topo.addr(d, core) for d, _ in to]
-        dsts = [what(k, n) for _, k in to]
-        if len(to) == 1:
-            g.remote_dma(out_ap=dsts[0], in_ap=what(a, n), remote_sem=sem, local_sem=s.sent, pid=ids[0][1],
-                         routing_id=ids[0][0], dma_engine_mask=mask)
-        else:
-            g.remote_dma_fused([RemoteDMATransfer(dst_ids=[DstId(rid=r, pnc=p) for r, p in ids], dma_engine_mask=mask,
-                                                  remote_sem=sem, srcs=[what(a, n)], dsts=dsts)], local_sem=s.sent)
-        engines = bin(mask).count("1")
-        sends[0] += engines
-        return engines
-
+    cable, switch = topo.mask(core, peer), topo.mask(core, near[1]) & topo.mask(core, near[2]) & topo.mask(core, near[3])
+    away = topo.mask(helper_of(near[3], topo), core)
+    away5 = topo.mask(helper_of(far[1], topo), core)
+    n3, n5 = bin(away).count("1"), bin(away5).count("1")
     g.wait_ge(s.vq, 1)
-    ec = put(planes, 0, 1, [(peer, 4)], s.rp4)
-    put(codes, 0, 1, [(peer, 4)], s.rc4)
-    es = put(codes, 0, 1, [(near[1], 1), (near[2], 2)], s.rc12)
+    ec = send(g, core, topo, s.rp4, s.sent, planes(0), [(peer, planes(4))], cable)
+    send(g, core, topo, s.rc4, s.sent, codes(0), [(peer, codes(4))], cable)
+    eh = send(g, core, topo, s.rh, s.sent, codes(0), [(helper, T.HQ[:, 0:C].bitcast(dt.uint8))],
+              chip_mask(core, helper, peer, topo))
+    es = send(g, core, topo, s.rc12, s.sent, codes(0), [(near[1], codes(1)), (near[2], codes(2))], switch)
     g.wait_ge(s.rp4, ec)
-    put(planes, 0, 2, [(near[1], 1)], s.rp1)
+    send(g, core, topo, s.rp, s.sent, planes(0, 2), [(near[k], planes(k, 2)) for k in (1, 2, 3)], switch)
     g.wait_ge(s.rc4, ec)
-    put(codes, 0, 2, [(near[3], 3)], s.rm3)
-    g.wait_ge(s.rc12, 2 * es)
-    put(codes, 1, 1, [(peer, 5)], s.rk5)
-    g.wait_ge(s.rp1, es)
-    put(planes, 0, 4, [(near[2], 2)], s.rp3)
-    put(codes, 4, 1, [(near[2], 6)], s.rr6)
+    send(g, core, topo, s.rc67, s.sent, codes(4), [(near[2], codes(6)), (near[3], codes(7))], switch)
     g.sem_inc(s.issued, 1)
-    g.wait_ge(s.sent, sends[0])
+    g.wait_ge(s.sent, 2 * ec + eh + 3 * es)
 
     def product(k):
-        q, p = QP[k], PP[k]
-        g.tensor.matmul_mx(T.ps[:, bank(k):bank(k) + C], T.Q[:, q * C:(q + 1) * C], T.P[:, p * C:(p + 1) * C],
+        p = PP[k]
+        g.tensor.matmul_mx(T.ps[:, bank(k):bank(k) + C], T.Q[:, k * C:(k + 1) * C], T.P[:, p * C:(p + 1) * C],
                            T.XQ[:, :], T.XP[:, :], True, True).then_inc(s["m%d" % k], 1)
 
     g.tensor.wait_ge(s.vq, 1)
@@ -143,23 +173,22 @@ def rank_program(g, core, T, topo):
     g.tensor.wait_ge(s.rp4, ec)
     g.tensor.wait_ge(s.rc4, ec)
     product(4)
-    g.tensor.wait_ge(s.rp1, es)
+    g.tensor.wait_ge(s.rp, 3 * es)
     g.tensor.wait_ge(s.rc12, 2 * es)
     product(1)
-    g.tensor.wait_ge(s.rk5, ec)
-    product(5)
-    g.tensor.wait_ge(s.rm3, es)
-    g.tensor.wait_ge(s.rp3, es)
     product(2)
+    g.tensor.wait_ge(s.rc5, n5)
+    product(5)
+    g.tensor.wait_ge(s.rc3, n3)
     product(3)
-    product(7)
-    g.tensor.wait_ge(s.rr6, es)
+    g.tensor.wait_ge(s.rc67, 2 * es)
     product(6)
+    product(7)
 
     ready = {k: n for n in STORES for k in STORES[n]}
-    for k in (0, 4, 1, 5, 2, 3, 7, 6):
+    for k in (0, 4, 1, 2, 5, 3, 6, 7):
         a, b = yblk(k)
-        if k in (0, 1, 2, 6):
+        if k in (0, 1, 5, 6):
             g.vector.wait_ge(s["m%d" % k], 1)
             g.vector.tensor_copy(T.Y[:, a:b], T.ps[:, bank(k):bank(k) + C]).then_inc(s[ready[k]], 1)
         else:

from concourse.bass import DstId, RemoteDMATransfer
from concourse.mybir import dt, AluOpType, ActivationFunctionType

C = 128
W4 = 4 * C
NT = 8
WORLD = 512
LR = 2.0 ** -3
PP = {0: 0, 4: 1, 1: 2, 5: 3, 2: 4, 6: 5, 3: 6, 7: 7}
STORES = {"y01": [0, 1], "y45": [4, 5], "y23": [2, 3], "y67": [6, 7]}

SCRATCH = {
    "Z": ("sbuf", [128, W4 + 8], "bfloat16"),
    "SQ": ("sbuf", [128, 4 * C], "float8_e4m3fn_x4"),
    "SP": ("sbuf", [128, 4 * C], "uint8"),
    "WQ": ("sbuf", [128, C], "float8_e4m3fn_x4"),
    "WP": ("sbuf", [128, C], "uint8"),
    "G": ("sbuf", [128, W4], "bfloat16"),
    "G8": ("sbuf", [128, W4], "bfloat16"),
    "H": ("sbuf", [128, W4], "bfloat16"),
    "XT": ("sbuf", [128, W4], "bfloat16"),
    "XQ": ("sbuf", [128, C], "float8_e4m3fn_x4"),
    "XP": ("sbuf", [128, C], "uint8"),
    "Q": ("sbuf", [128, NT * C], "float8_e4m3fn_x4"),
    "P": ("sbuf", [128, NT * C], "uint8"),
    "HQ": ("sbuf", [128, C], "float8_e4m3fn_x4"),
    "Y": ("sbuf", [128, NT * C], "float32"),
    "ps": ("psum", [128, NT * 512], "float32"),
}
SEMAPHORES = (["z0", "z1", "z2", "lw", "lg", "lx", "h", "vq", "xq", "sent", "issued", "stored",
               "rp4", "rp", "rc4", "rc12", "rc3", "rc5", "rc67", "rh"] + list(STORES)
              + [n + "%d" % b for n in ("sq", "d", "g") for b in range(4)] + ["m%d" % k for k in range(NT)])


def rack_group(core, T, topo):
    def at(same_host, same_chip):
        return [c for c in T.cores if topo.rack(topo.host(c)) == topo.rack(topo.host(core))
                and (topo.host(c) == topo.host(core)) == same_host
                and (topo.chip(c) == topo.chip(core)) == same_chip][0]
    return [at(True, True), at(True, False), at(False, True), at(False, False)]


def peer_of(core, T, topo):
    return [c for c in T.cores if topo.rack(topo.host(c)) != topo.rack(topo.host(core))
            and topo.chip(c) == topo.chip(core) and topo.may_write(core, c)][0]


def helper_of(core, topo):
    return [c for c in range(WORLD) if topo.host(c) == topo.host(core) and topo.chip(c) == topo.chip(core)
            and topo.die(c) != topo.die(core)][0]


def send(g, core, topo, sem, local, src, to, mask):
    ids = [topo.addr(d, core) for d, _ in to]
    dsts = [ap for _, ap in to]
    if len(to) == 1:
        g.remote_dma(out_ap=dsts[0], in_ap=src, remote_sem=sem, local_sem=local, pid=ids[0][1],
                     routing_id=ids[0][0], dma_engine_mask=mask)
    else:
        g.remote_dma_fused([RemoteDMATransfer(dst_ids=[DstId(rid=r, pnc=p) for r, p in ids], dma_engine_mask=mask,
                                              remote_sem=sem, srcs=[src], dsts=dsts)], local_sem=local)
    return bin(mask).count("1")


def chip_mask(core, helper, away, topo):
    return topo.mask(core, helper) & ~topo.mask(core, away)


def helper_program(g, core, owner, T, topo):
    s = T.sem
    near = rack_group(owner, T, topo)
    far = rack_group(peer_of(owner, T, topo), T, topo)
    g.wait_ge(s.rh, bin(chip_mask(owner, core, far[0], topo)).count("1"))
    src = T.HQ[:, 0:C].bitcast(dt.uint8)
    n = 0
    for to, k, sem in ((far[1], 5, s.rc5), (near[3], 3, s.rc3)):
        n += send(g, core, topo, sem, s.sent, src, [(to, T.Q[:, k * C:(k + 1) * C].bitcast(dt.uint8))],
                  topo.mask(core, to))
    g.wait_ge(s.sent, n)


def rank_program(g, core, T, topo):
    rank = T.rank_of(core)
    if rank is None:
        for c in T.cores:
            if topo.host(c) == topo.host(core) and topo.chip(c) == topo.chip(core) and helper_of(c, topo) == core:
                helper_program(g, core, c, T, topo)
        return
    s = T.sem
    near = rack_group(core, T, topo)
    peer = peer_of(core, T, topo)
    far = rack_group(peer, T, topo)
    helper = helper_of(core, topo)
    owner = near + far

    def codes(a):
        return T.Q[:, a * C:(a + 1) * C].bitcast(dt.uint8)

    def planes(a, n=1):
        return T.P[:, PP[a] * C:(PP[a] + n) * C]

    def yblk(k):
        r = T.rank_of(owner[k])
        return r * C, (r + 1) * C

    def bank(k):
        return ((k + 4) % NT) * 512

    g.sync.dma_start(T.WQ[:, 0:C].bitcast(dt.uint8), T.wc[:, :]).then_inc(s.lw, 16)
    g.sync.dma_start(T.WP[:, :], T.ws[:, :]).then_inc(s.lw, 16)
    g.sync.wait_ge(s.sq3, 1)
    g.sync.dma_start(T.XT[:, :], T.x[:, :]).then_inc(s.lx, 16)

    g.scalar.dma_start(T.G[:, :], T.gr[:, :]).then_inc(s.lg, 16)
    g.scalar.wait_ge(s.lg, 16)
    for b in range(4):
        g.scalar.activation(T.G8[:, b * C:(b + 1) * C], T.G[:, b:W4:4], ActivationFunctionType.Copy,
                            scale=LR).then_inc(s["g%d" % b], 1)

    g.vector.memset(T.Z[:, 3:3 + W4:4], 0.0).then_inc(s.z0, 1)
    for k in range(3):
        g.vector.memset(T.Z[:, k:W4 + 3:4], 0.0).then_inc(s.z2, 1)
    g.wait_ge(s.z0, 1)
    g.affine_select(T.Z[:, 3:3 + W4:4], T.Z[:, 3:3 + W4:4], [[-1, C]], AluOpType.not_equal, 1.0, 0, 1).then_inc(s.z1, 1)
    g.vector.wait_ge(s.z2, 3)
    g.vector.wait_ge(s.z1, 1)
    for b in range(4):
        g.vector.quantize_mx(T.SQ[:, b * C:(b + 1) * C], T.SP[:, b * C:(b + 1) * C],
                             T.Z[:, 3 - b:3 - b + W4]).then_inc(s["sq%d" % b], 1)

    g.tensor.wait_ge(s.lw, 32)
    for b in range(4):
        g.tensor.wait_ge(s["sq%d" % b], 1)
        g.tensor.matmul_mx(T.ps[:, b * 512:b * 512 + C], T.SQ[:, b * C:(b + 1) * C], T.SP[:, b * C:(b + 1) * C],
                           T.WQ[:, 0:C], T.WP[:, 0:C], True, True).then_inc(s["d%d" % b], 1)

    for b in range(4):
        g.vector.wait_ge(s["d%d" % b], 1)
        g.vector.wait_ge(s["g%d" % b], 1)
        g.vector.tensor_tensor(T.H[:, b:W4:4], T.ps[:, b * 512:b * 512 + C], T.G8[:, b * C:(b + 1) * C],
                               AluOpType.subtract).then_inc(s.h, 1)
    g.vector.wait_ge(s.h, 4)
    g.vector.quantize_mx(T.Q[:, 0:C], planes(0), T.H[:, :]).then_inc(s.vq, 1)
    g.vector.wait_ge(s.lx, 16)
    g.vector.quantize_mx(T.XQ[:, :], T.XP[:, :], T.XT[:, :]).then_inc(s.xq, 1)

    cable, switch = topo.mask(core, peer), topo.mask(core, near[1]) & topo.mask(core, near[2]) & topo.mask(core, near[3])
    away = topo.mask(helper_of(near[3], topo), core)
    away5 = topo.mask(helper_of(far[1], topo), core)
    n3, n5 = bin(away).count("1"), bin(away5).count("1")
    g.wait_ge(s.vq, 1)
    ec = send(g, core, topo, s.rp4, s.sent, planes(0), [(peer, planes(4))], cable)
    send(g, core, topo, s.rc4, s.sent, codes(0), [(peer, codes(4))], cable)
    eh = send(g, core, topo, s.rh, s.sent, codes(0), [(helper, T.HQ[:, 0:C].bitcast(dt.uint8))],
              chip_mask(core, helper, peer, topo))
    es = send(g, core, topo, s.rc12, s.sent, codes(0), [(near[1], codes(1)), (near[2], codes(2))], switch)
    g.wait_ge(s.rp4, ec)
    send(g, core, topo, s.rp, s.sent, planes(0, 2), [(near[k], planes(k, 2)) for k in (1, 2, 3)], switch)
    g.wait_ge(s.rc4, ec)
    send(g, core, topo, s.rc67, s.sent, codes(4), [(near[2], codes(6)), (near[3], codes(7))], switch)
    g.sem_inc(s.issued, 1)
    g.wait_ge(s.sent, 2 * ec + eh + 3 * es)

    def product(k):
        p = PP[k]
        g.tensor.matmul_mx(T.ps[:, bank(k):bank(k) + C], T.Q[:, k * C:(k + 1) * C], T.P[:, p * C:(p + 1) * C],
                           T.XQ[:, :], T.XP[:, :], True, True).then_inc(s["m%d" % k], 1)

    g.tensor.wait_ge(s.vq, 1)
    g.tensor.wait_ge(s.xq, 1)
    product(0)
    g.tensor.wait_ge(s.h, 4)
    g.tensor.wait_ge(s.rp4, ec)
    g.tensor.wait_ge(s.rc4, ec)
    product(4)
    g.tensor.wait_ge(s.rp, 3 * es)
    g.tensor.wait_ge(s.rc12, 2 * es)
    product(1)
    product(2)
    g.tensor.wait_ge(s.rc5, n5)
    product(5)
    g.tensor.wait_ge(s.rc3, n3)
    product(3)
    g.tensor.wait_ge(s.rc67, 2 * es)
    product(6)
    product(7)

    ready = {k: n for n in STORES for k in STORES[n]}
    for k in (0, 4, 1, 2, 5, 3, 6, 7):
        a, b = yblk(k)
        if k in (0, 1, 5, 6):
            g.vector.wait_ge(s["m%d" % k], 1)
            g.vector.tensor_copy(T.Y[:, a:b], T.ps[:, bank(k):bank(k) + C]).then_inc(s[ready[k]], 1)
        else:
            g.scalar.wait_ge(s["m%d" % k], 1)
            g.scalar.activation(T.Y[:, a:b], T.ps[:, bank(k):bank(k) + C],
                                ActivationFunctionType.Copy).then_inc(s[ready[k]], 1)

    g.sync.wait_ge(s.issued, 1)
    for n in STORES:
        cols = [yblk(k) for k in STORES[n]]
        a, b = min(c[0] for c in cols), max(c[1] for c in cols)
        g.sync.wait_ge(s[n], len(cols))
        g.sync.dma_start(T.y[:, a:b], T.Y[:, a:b]).then_inc(s.stored, 16)
    g.sync.wait_ge(s.stored, 16 * len(STORES))
